import numpy as np
import ml_dtypes


def mxq(x, axis, fmt="e4m3"):
    dtype, down = {"e4m3": (ml_dtypes.float8_e4m3fn, 7), "e5m2": (ml_dtypes.float8_e5m2, 14)}[fmt]
    v = np.moveaxis(np.asarray(x, np.float32).astype(ml_dtypes.bfloat16).astype(np.float64), axis, -1)
    blocks = v.reshape(v.shape[:-1] + (-1, 32))
    amax = np.abs(blocks).max(-1, keepdims=True)
    byte = np.maximum(np.where(amax > 0, np.frexp(amax)[1] - 1 + 127, 0) - down, 1)
    scale = np.exp2(byte - 127.0)
    codes = (blocks / scale).astype(np.float32).astype(dtype).astype(np.float64)
    return np.moveaxis((codes * scale).reshape(v.shape), -1, axis)


WIDE = False


def mx_kscale(k):
    if not WIDE:
        return np.ones(k)
    levels = np.array([10, -10, 5, -5, 0])
    if k % 512:
        return np.exp2(np.random.permutation(np.resize(levels, k // 32))).repeat(32)
    a = np.empty((k // 512, 16))
    for p in range(k // 512):
        a[p, :8] = np.random.permutation(np.resize(levels, 8))
        for g in range(8):
            far = levels[np.abs(levels - a[p, g]) >= 10]
            a[p, g + 8] = far[np.random.randint(len(far))]
    return np.exp2(a.ravel()).repeat(32)


def f64(x):
    return np.asarray(x).astype(np.float64)


def striped(idx):
    return np.tile(idx.reshape(-1, 16).T, (8, 1)).astype(np.uint16)


def unstriped(offs):
    return offs[:16].T.reshape(-1).astype(np.int64)


E2M1 = np.array([0.0, 0.5, 1.0, 1.5, 2.0, 3.0, 4.0, 6.0, -0.0, -0.5, -1.0, -1.5, -2.0, -3.0, -4.0, -6.0])


def pack_weight(w, fmt):
    k, n = w.shape
    w = f64(np.asarray(w, np.float32).astype(ml_dtypes.bfloat16)).reshape(k // 32, 32, n)
    amax = np.abs(w).max(1)
    if fmt == "e4m3":
        byte = np.frexp(amax)[1] - 1 + 127 - 7
    else:
        mant, ex = np.frexp(amax / 6.0)
        byte = np.where(mant > 0.5, ex, ex - 1) + 127
    byte = np.clip(np.where(amax > 0, byte, 1), 1, 254)
    scaled = (w * np.exp2(127.0 - byte)[:, None, :]).reshape(k, n).astype(np.float32)
    by_word = np.ascontiguousarray(scaled.reshape(k // 512, 128, 4, n).transpose(0, 1, 3, 2))
    if fmt == "e4m3":
        words = by_word.astype(ml_dtypes.float8_e4m3fn).view(np.uint8)
    else:
        c = by_word.astype(ml_dtypes.float4_e2m1fn).view(np.uint8) & 0xF
        words = (c[..., 0::2] | (c[..., 1::2] << 4)).reshape(k // 512, 128, 2 * n)
    return np.ascontiguousarray(words), np.ascontiguousarray(byte.astype(np.uint8).reshape(k // 512, 16, n))


def unpack_weight(words, scales, fmt):
    g, _, n = scales.shape
    words = np.ascontiguousarray(words).reshape(g, 128, n, -1)
    if fmt == "e4m3":
        vals = words.view(ml_dtypes.float8_e4m3fn).astype(np.float64)
    else:
        nib = np.empty((g, 128, n, 4), np.uint8)
        nib[..., 0::2] = words & 0xF
        nib[..., 1::2] = words >> 4
        vals = E2M1[nib]
    vals = vals * np.repeat(np.exp2(scales.astype(np.float64) - 127.0), 8, axis=1)[..., None]
    return vals.transpose(0, 1, 3, 2).reshape(g * 512, n)


def gelu(v):
    return 0.5 * v * (1.0 + np.tanh(np.sqrt(2.0 / np.pi) * (v + 0.044715 * v**3)))


def often(T, S):
    return np.random.permutation(T)[(T * np.random.uniform(0, 1, S) ** 4).astype(np.int64)]


def bf(x):
    return np.asarray(x, np.float32).astype(ml_dtypes.bfloat16)


def planes(Y):
    n, m = Y.shape
    b = f64(bf(Y)).reshape(n // 32, 32, m)
    amax = np.abs(b).max(1)
    byte = np.clip(np.where(amax > 0, np.frexp(amax)[1] - 1 + 127 - 7, 1), 1, 254)
    codes = (b * np.exp2(127.0 - byte)[:, None, :]).reshape(n, m).astype(np.float32).astype(ml_dtypes.float8_e4m3fn).view(np.uint8)
    words = codes.reshape(n // 512, 128, 4, m).transpose(0, 1, 3, 2)
    return np.ascontiguousarray(words), np.ascontiguousarray(byte.astype(np.uint8).reshape(n // 512, 16, m))


K, K2, H, N, T, S, P = 1024, 512, 1024, 1024, 4096, 1024, 512

def setup_inputs():
    n = np.random.standard_normal
    s, s2, u = mx_kscale(K)[:, None], mx_kscale(K2)[:, None], mx_kscale(H)[:, None]
    d = {}
    d["tab_words"], d["tab_scales"] = pack_weight(n((K, T)) * s, "e4m3")
    d["tab2_words"], d["tab2_scales"] = pack_weight(n((K2, T)) * s2, "e4m3")
    d["tab3_words"], d["tab3_scales"] = pack_weight(n((K2, T)) * s2, "e4m3")
    d["offs"] = striped(np.random.permutation(T)[:S])
    d["offs2"] = striped(np.random.permutation(T)[:S])
    d["offs3"] = striped(np.random.permutation(T)[:S])
    d["pos1"] = striped(np.random.permutation(S)[:P])
    d["pos2"] = striped(often(S, P))
    d["pos3"] = striped(often(S, P))
    d["w1"] = (n((K, H)) / K ** 0.5 / s * u.T).astype(np.float32)
    d["w2_words"], d["w2_scales"] = pack_weight(n((K2, H)) / K2 ** 0.5 / s2 * u.T, "e2m1")
    d["w3"] = (n((K2, H)) / K2 ** 0.5 / s2 * u.T).astype(np.float32)
    d["w4_words"], d["w4_scales"] = pack_weight(n((H, N)) / H ** 0.5 / u * np.exp(0.8 * n(N)), "e4m3")
    return d

def reference(tab_words, tab_scales, tab2_words, tab2_scales, tab3_words, tab3_scales, offs, offs2, offs3,
              pos1, pos2, pos3, w1, w2_words, w2_scales, w3, w4_words, w4_scales):
    v = unpack_weight(tab_words, tab_scales, "e4m3")[:, unstriped(offs)]
    v2 = unpack_weight(tab2_words, tab2_scales, "e4m3")[:, unstriped(offs2)]
    v3 = unpack_weight(tab3_words, tab3_scales, "e4m3")[:, unstriped(offs3)]
    a = mxq(f64(w1), 0, "e4m3").T @ v
    b = unpack_weight(w2_words, w2_scales, "e2m1").T @ v2
    d = mxq(f64(w3), 0, "e4m3").T @ v3
    aj = a[:, unstriped(pos1)]
    bj = b[:, unstriped(pos2)]
    dj = d[:, unstriped(pos3)]
    high = np.maximum(np.maximum(aj, bj), dj)
    low = np.minimum(np.minimum(aj, bj), dj)
    z = mxq(high - low, 0, "e4m3")
    y = unpack_weight(w4_words, w4_scales, "e4m3").T @ z
    words, scales = planes(y)
    return y, words, scales

@@ -1,0 +1,243 @@
+from contextlib import ExitStack
+
+import concourse.mybir as mybir
+
+K, K2, H, N, T, S, TESTS = 1024, 512, 1024, 1024, 4096, 1024, 512
+FLOPS = 2 * (K + 2 * K2) * H * S + 2 * H * N * TESTS
+
+F32 = mybir.dt.float32
+BF16 = mybir.dt.bfloat16
+I32 = mybir.dt.int32
+U32 = mybir.dt.uint32
+U16 = mybir.dt.uint16
+U8 = mybir.dt.uint8
+FP8X4 = mybir.dt.float8_e4m3fn_x4
+FP4X4 = mybir.dt.float4_e2m1fn_x4
+ALU = mybir.AluOpType
+
+P = 128
+PACK = 4
+GROUP = P * PACK
+BANK = 512
+HALF = TESTS // 2
+
+
+def tile_list_chronometer_spread_features_kernel(
+    tc, tab_words, tab_scales, tab2_words, tab2_scales, tab3_words, tab3_scales, offs, offs2, offs3,
+    pos1, pos2, pos3, w1, w2_words, w2_scales, w3, w4_words, w4_scales, out_0, out_1, out_2,
+):
+    nc = tc.nc
+    with ExitStack() as ctx:
+        keep = ctx.enter_context(tc.tile_pool(name="keep", bufs=1))
+        big = ctx.enter_context(tc.tile_pool(name="big", bufs=4))
+        ring = ctx.enter_context(tc.tile_pool(name="ring", bufs=4))
+        rounded = ctx.enter_context(tc.tile_pool(name="rounded", bufs=3))
+        reading = ctx.enter_context(tc.tile_pool(name="reading", bufs=8))
+        work = ctx.enter_context(tc.tile_pool(name="work", bufs=2))
+        psum = ctx.enter_context(tc.psum_pool(name="psum", bufs=4))
+
+        def load_list(name, source):
+            tile = keep.tile(list(source.shape), U16, name=name)
+            nc.sync.dma_start(tile[:], source)
+            return tile
+
+        def load_table_words(source):
+            tile = big.tile([P, T], U32, name="big", align_bytes=64)
+            nc.sync.dma_start(tile[:].bitcast(I32), source.rearrange("p t i -> p (t i)").bitcast(I32))
+            return tile
+
+        def zeroed_plane(name, width):
+            tile = keep.tile([P, width], U8, name=name, align_bytes=64)
+            nc.vector.memset(tile[:].bitcast(I32), 0)
+            return tile
+
+        def load_scale_rows(queue, tile, first_row, source):
+            rows = 4 * source.shape[0]
+            for q in range(4):
+                queue.dma_start(
+                    tile[32 * q + first_row : 32 * q + first_row + rows, :].bitcast(I32),
+                    source[:, 4 * q : 4 * q + 4, :].bitcast(I32),
+                )
+
+        def load_weight_block(source, a, g):
+            tile = ring.tile([P, PACK, GROUP], F32, name="ring", align_bytes=64)
+            rows = source[GROUP * a : GROUP * (a + 1), GROUP * g : GROUP * (g + 1)]
+            nc.sync.dma_start(tile[:], rows.rearrange("(p j) c -> p j c", j=PACK))
+            return tile
+
+        def gather(name, dtype, table, offsets):
+            picked = keep.tile([P, S], dtype, name=name, align_bytes=64)
+            nc.vector.tensor_copy(picked[:], table[:].indirect(offsets[:]))
+            return picked
+
+        def quantize(name, values, width):
+            codes = keep.tile([P, width], U32, name=name + "_codes", align_bytes=64)
+            scales = keep.tile([P, width], U8, name=name + "_scales", align_bytes=64)
+            nc.vector.quantize_mx(out=codes[:].bitcast(FP8X4), scales=scales[:], in_=values)
+            return codes, scales
+
+        def quantize_weight_block(name, raw):
+            dealt = rounded.tile([P, PACK * GROUP], BF16, name="rounded", align_bytes=64)
+            nc.scalar.copy(
+                dealt[:].rearrange("p (t m j) -> p m t j", t=PACK, j=PACK),
+                raw[:].rearrange("p j (m t) -> p m t j", t=PACK),
+            )
+            return quantize(name, dealt[:], GROUP)
+
+        def first_stage(passes):
+            result = reading.tile([P, S], F32, name="reading", align_bytes=64)
+            for c in range(S // BANK):
+                cols = slice(BANK * c, BANK * (c + 1))
+                acc = psum.tile([P, BANK], F32, name="first")
+                for i, (codes, scales, words, plane) in enumerate(passes):
+                    nc.tensor.matmul_mx(
+                        out=acc[:], lhsT=codes, lhsT_scale=scales,
+                        rhs=words[:, cols].bitcast(FP8X4), rhs_scale=plane[:, cols],
+                        start=(i == 0), stop=(i == len(passes) - 1),
+                    )
+                nc.scalar.copy(result[:, cols], acc[:])
+            return result
+
+        def round_interleaved(values, width):
+            grouped = rounded.tile([P, PACK * width], BF16, name="rounded", align_bytes=64)
+            return grouped, (
+                grouped[:].rearrange("p (c i t) -> p c t i", i=4, t=PACK),
+                values.rearrange("p t (c i) -> p c t i", i=4),
+            )
+
+        tab2_plane = zeroed_plane("tab2_plane", T)
+        weight_plane = zeroed_plane("weight_plane", H)
+        tab3_plane = zeroed_plane("tab3_plane", T)
+        tab_plane = zeroed_plane("tab_plane", T)
+        w4_plane = zeroed_plane("w4_plane", N)
+
+        offs2_t = load_list("offs2_t", offs2)
+        offs3_t = load_list("offs3_t", offs3)
+        w2_raw = keep.tile([P, 2 * H], U8, name="w2_raw", align_bytes=64)
+        nc.sync.dma_start(w2_raw[:].bitcast(I32), w2_words[0].bitcast(I32))
+        tab2_t = load_table_words(tab2_words[0])
+        load_scale_rows(nc.scalar, tab2_plane, 0, tab2_scales)
+        load_scale_rows(nc.scalar, weight_plane, 0, w2_scales)
+        load_scale_rows(nc.scalar, tab3_plane, 0, tab3_scales)
+        tab3_t = load_table_words(tab3_words[0])
+        pos2_t = load_list("pos2_t", pos2)
+        w3_raw = [load_weight_block(w3, 0, g) for g in range(2)]
+        tab_t = [load_table_words(tab_words[a]) for a in range(2)]
+        offs_t = load_list("offs_t", offs)
+        pos3_t = load_list("pos3_t", pos3)
+        pos1_t = load_list("pos1_t", pos1)
+        load_scale_rows(nc.sync, tab_plane, 0, tab_scales)
+        w1_raw = {(a, 0): load_weight_block(w1, a, 0) for a in range(2)}
+
+        w2_dealt = keep.tile([P, 2 * H], U8, name="w2_dealt", align_bytes=64)
+        nc.vector.tensor_copy(
+            w2_dealt[:].rearrange("p (g t m e) -> p g t m e", g=2, t=PACK, e=2),
+            w2_raw[:].rearrange("p (g m t e) -> p g t m e", g=2, t=PACK, e=2),
+        )
+        v2_plane = gather("v2_plane", U8, tab2_plane, offs2_t)
+        v2_words = gather("v2_words", U32, tab2_t, offs2_t)
+        dealt_plane = keep.tile([P, H], U8, name="dealt_plane", align_bytes=64)
+        nc.vector.tensor_copy(
+            dealt_plane[:].rearrange("p (g t m) -> p g t m", g=2, t=PACK),
+            weight_plane[:].rearrange("p (g m t) -> p g t m", g=2, t=PACK),
+        )
+        v3_plane = gather("v3_plane", U8, tab3_plane, offs3_t)
+        v3_words = gather("v3_words", U32, tab3_t, offs3_t)
+
+        b_picked = big.tile([P, 8, TESTS], F32, name="big", align_bytes=64)
+        for i in range(8):
+            b = first_stage([(
+                w2_dealt[:, 2 * P * i : 2 * P * (i + 1)].bitcast(FP4X4), dealt_plane[:, P * i : P * (i + 1)],
+                v2_words, v2_plane,
+            )])
+            nc.vector.tensor_copy(b_picked[:, i, :], b[:].indirect(pos2_t[:]))
+
+        w3_q = [quantize_weight_block("w3_%d" % g, w3_raw[g]) for g in range(2)]
+        for a in range(2):
+            w1_raw[(a, 1)] = load_weight_block(w1, a, 1)
+        v_words = [gather("v_words_%d" % a, U32, tab_t[a], offs_t) for a in range(2)]
+        v_plane = gather("v_plane", U8, tab_plane, offs_t)
+        d_less_b = big.tile([P, 8, TESTS], F32, name="big", align_bytes=64)
+        for i in range(8):
+            g, t = divmod(i, PACK)
+            cols = slice(P * t, P * (t + 1))
+            d = first_stage([(w3_q[g][0][:, cols].bitcast(FP8X4), w3_q[g][1][:, cols], v3_words, v3_plane)])
+            nc.vector.tensor_tensor(d_less_b[:, i, :], d[:].indirect(pos3_t[:]), b_picked[:, i, :], ALU.subtract)
+
+        readings = []
+        for g in range(2):
+            w1_q = [quantize_weight_block("w1_%d_%d" % (a, g), w1_raw[(a, g)]) for a in range(2)]
+            for t in range(PACK):
+                cols = slice(P * t, P * (t + 1))
+                readings.append(first_stage([
+                    (w1_q[a][0][:, cols].bitcast(FP8X4), w1_q[a][1][:, cols], v_words[a], v_plane[4 * a :, :])
+                    for a in range(2)
+                ]))
+
+        w4_raw = ring.tile([P, 2, N], I32, name="ring", align_bytes=64)
+        nc.sync.dma_start(w4_raw[:], w4_words.rearrange("a p c i -> p a (c i)").bitcast(I32))
+        load_scale_rows(nc.sync, w4_plane, 0, w4_scales)
+        w4_dealt_plane = keep.tile([P, N], U8, name="w4_dealt_plane", align_bytes=64)
+        nc.vector.tensor_copy(
+            w4_dealt_plane[:].rearrange("p (g t m) -> p g t m", g=2, t=PACK),
+            w4_plane[:].rearrange("p (g m t) -> p g t m", g=2, t=PACK),
+        )
+        w4_dealt = keep.tile([P, 2 * N], I32, name="w4_dealt", align_bytes=64)
+        nc.vector.tensor_copy(
+            w4_dealt[:].rearrange("p (b t m i) -> p b m t i", b=4, t=PACK, i=4),
+            w4_raw[:].rearrange("p a (g m i t) -> p (a g) m t i", g=2, i=4, t=PACK),
+        )
+
+        y_codes = keep.tile([P, 2, TESTS], U32, name="y_codes", align_bytes=64)
+        y_scales = keep.tile([P, 2, TESTS], U8, name="y_scales", align_bytes=64)
+        for h in range(2):
+            tests = slice(HALF * h, HALF * (h + 1))
+            banks = [psum.tile([P, 2, HALF], F32, name="second") for i in range(4)]
+            for g in range(2):
+                a_less_b = work.tile([P, PACK, HALF], F32, name="a_less_b", align_bytes=64)
+                for t in range(PACK):
+                    i = PACK * g + t
+                    nc.vector.tensor_tensor(
+                        a_less_b[:, t, :], readings[i][:].indirect(pos1_t[:, 16 * h : 16 * (h + 1)]),
+                        b_picked[:, i, tests], ALU.subtract,
+                    )
+                other = d_less_b[:, PACK * g : PACK * (g + 1), tests]
+                high = work.tile([P, PACK, HALF], F32, name="high", align_bytes=64)
+                nc.vector.scalar_tensor_tensor(high[:], a_less_b[:], 0.0, other, ALU.max, ALU.max)
+                nc.vector.scalar_tensor_tensor(a_less_b[:], a_less_b[:], 0.0, other, ALU.min, ALU.min)
+                nc.vector.tensor_tensor(high[:], high[:], a_less_b[:], ALU.subtract)
+                grouped, views = round_interleaved(high[:], HALF)
+                nc.scalar.copy(*views)
+                z_codes, z_scales = quantize("z_%d_%d" % (h, g), grouped[:], HALF)
+                for i in range(8):
+                    nc.tensor.matmul_mx(
+                        out=banks[i // 2][:, i % 2, :],
+                        lhsT=w4_dealt[:, N * g + P * i : N * g + P * (i + 1)].bitcast(FP8X4),
+                        lhsT_scale=w4_dealt_plane[4 * g :, P * i : P * (i + 1)],
+                        rhs=z_codes[:].bitcast(FP8X4), rhs_scale=z_scales[:],
+                        start=(g == 0 and i % 2 == 0), stop=(g == 1 and i % 2 == 1),
+                    )
+            y = ring.tile([P, 8, HALF], F32, name="ring", align_bytes=64)
+            for g in range(2):
+                for i in (2 * g, 2 * g + 1):
+                    nc.scalar.copy(y[:, 2 * i : 2 * i + 2, :], banks[i][:])
+                y_group = y[:, PACK * g : PACK * (g + 1), :]
+                nc.sync.dma_start(
+                    out_0[GROUP * g : GROUP * (g + 1), tests].rearrange("(p t) j -> p t j", t=PACK), y_group
+                )
+                grouped, views = round_interleaved(y_group, HALF)
+                if h == 0:
+                    nc.scalar.copy(*views)
+                else:
+                    nc.vector.tensor_copy(*views)
+                nc.vector.quantize_mx(
+                    out=y_codes[:, g, tests].bitcast(FP8X4), scales=y_scales[:, g, tests], in_=grouped[:]
+                )
+                nc.sync.dma_start(
+                    out_1[g, :, tests, :].rearrange("p m t -> p (m t)").bitcast(I32), y_codes[:, g, tests].bitcast(I32)
+                )
+        for q in range(4):
+            nc.sync.dma_start(
+                out_2[:, 4 * q : 4 * q + 4, :].rearrange("g r m -> r g m").bitcast(I32),
+                y_scales[32 * q : 32 * q + 4, :, :].bitcast(I32),
+            )

@@ -1,6 +1,7 @@
 from contextlib import ExitStack
 
 import concourse.mybir as mybir
+from concourse.masks import make_identity
 
 K, K2, H, N, T, S, TESTS = 1024, 512, 1024, 1024, 4096, 1024, 512
 FLOPS = 2 * (K + 2 * K2) * H * S + 2 * H * N * TESTS
@@ -14,12 +15,13 @@ U8 = mybir.dt.uint8
 FP8X4 = mybir.dt.float8_e4m3fn_x4
 FP4X4 = mybir.dt.float4_e2m1fn_x4
 ALU = mybir.AluOpType
+RELU = mybir.ActivationFunctionType.Relu
 
 P = 128
 PACK = 4
 GROUP = P * PACK
 BANK = 512
-HALF = TESTS // 2
+PIECES = (256, 128, 128)
 
 
 def tile_list_chronometer_spread_features_kernel(
@@ -29,7 +31,7 @@ def tile_list_chronometer_spread_features_kernel(
     nc = tc.nc
     with ExitStack() as ctx:
         keep = ctx.enter_context(tc.tile_pool(name="keep", bufs=1))
-        big = ctx.enter_context(tc.tile_pool(name="big", bufs=4))
+        big = ctx.enter_context(tc.tile_pool(name="big", bufs=1))
         ring = ctx.enter_context(tc.tile_pool(name="ring", bufs=4))
         rounded = ctx.enter_context(tc.tile_pool(name="rounded", bufs=3))
         reading = ctx.enter_context(tc.tile_pool(name="reading", bufs=8))
@@ -41,8 +43,8 @@ def tile_list_chronometer_spread_features_kernel(
             nc.sync.dma_start(tile[:], source)
             return tile
 
-        def load_table_words(source):
-            tile = big.tile([P, T], U32, name="big", align_bytes=64)
+        def load_table_words(name, source):
+            tile = big.tile([P, T], U32, name=name, align_bytes=64)
             nc.sync.dma_start(tile[:].bitcast(I32), source.rearrange("p t i -> p (t i)").bitcast(I32))
             return tile
 
@@ -76,19 +78,29 @@ def tile_list_chronometer_spread_features_kernel(
             nc.vector.quantize_mx(out=codes[:].bitcast(FP8X4), scales=scales[:], in_=values)
             return codes, scales
 
-        def quantize_weight_block(name, raw):
-            dealt = rounded.tile([P, PACK * GROUP], BF16, name="rounded", align_bytes=64)
-            nc.scalar.copy(
-                dealt[:].rearrange("p (t m j) -> p m t j", t=PACK, j=PACK),
-                raw[:].rearrange("p j (m t) -> p m t j", t=PACK),
+        def interleave_views(values, width):
+            grouped = rounded.tile([P, PACK * width], BF16, name="rounded", align_bytes=64)
+            return grouped, (
+                grouped[:].rearrange("p (c i t) -> p c t i", i=4, t=PACK),
+                values.rearrange("p t (c i) -> p c t i", i=4),
             )
-            return quantize(name, dealt[:], GROUP)
 
-        def first_stage(passes):
-            result = reading.tile([P, S], F32, name="reading", align_bytes=64)
+        def quantize_weight_block(name, raw, copy):
+            grouped, views = interleave_views(raw[:], GROUP)
+            copy(*views)
+            return quantize(name, grouped[:], GROUP)
+
+        def turn(out, parts):
+            for i, part in enumerate(parts):
+                nc.tensor.matmul(
+                    out, lhsT=part, rhs=identity[:], is_transpose=True, start=(i == 0), stop=(i == len(parts) - 1)
+                )
+
+        def first_stage(passes, pool=reading, name="reading"):
+            result = pool.tile([P, S], F32, name=name, align_bytes=64)
             for c in range(S // BANK):
                 cols = slice(BANK * c, BANK * (c + 1))
-                acc = psum.tile([P, BANK], F32, name="first")
+                acc = psum.tile([P, BANK], F32, name="acc")
                 for i, (codes, scales, words, plane) in enumerate(passes):
                     nc.tensor.matmul_mx(
                         out=acc[:], lhsT=codes, lhsT_scale=scales,
@@ -98,16 +110,12 @@ def tile_list_chronometer_spread_features_kernel(
                 nc.scalar.copy(result[:, cols], acc[:])
             return result
 
-        def round_interleaved(values, width):
-            grouped = rounded.tile([P, PACK * width], BF16, name="rounded", align_bytes=64)
-            return grouped, (
-                grouped[:].rearrange("p (c i t) -> p c t i", i=4, t=PACK),
-                values.rearrange("p t (c i) -> p c t i", i=4),
-            )
+        identity = keep.tile([P, P], F32, name="identity")
+        make_identity(nc, identity[:])
 
         tab2_plane = zeroed_plane("tab2_plane", T)
-        weight_plane = zeroed_plane("weight_plane", H)
         tab3_plane = zeroed_plane("tab3_plane", T)
+        w2_plane = zeroed_plane("w2_plane", H)
         tab_plane = zeroed_plane("tab_plane", T)
         w4_plane = zeroed_plane("w4_plane", N)
 
@@ -115,68 +123,106 @@ def tile_list_chronometer_spread_features_kernel(
         offs3_t = load_list("offs3_t", offs3)
         w2_raw = keep.tile([P, 2 * H], U8, name="w2_raw", align_bytes=64)
         nc.sync.dma_start(w2_raw[:].bitcast(I32), w2_words[0].bitcast(I32))
-        tab2_t = load_table_words(tab2_words[0])
-        load_scale_rows(nc.scalar, tab2_plane, 0, tab2_scales)
-        load_scale_rows(nc.scalar, weight_plane, 0, w2_scales)
+        load_scale_rows(nc.sync, tab2_plane, 0, tab2_scales)
         load_scale_rows(nc.scalar, tab3_plane, 0, tab3_scales)
-        tab3_t = load_table_words(tab3_words[0])
+        load_scale_rows(nc.scalar, w2_plane, 0, w2_scales)
+        tab2_t = load_table_words("then_b", tab2_words[0])
+        w3_raw = [load_weight_block(w3, 0, 0)]
         pos2_t = load_list("pos2_t", pos2)
-        w3_raw = [load_weight_block(w3, 0, g) for g in range(2)]
-        tab_t = [load_table_words(tab_words[a]) for a in range(2)]
+        tab3_t = load_table_words("then_d", tab3_words[0])
+        w3_raw.append(load_weight_block(w3, 0, 1))
         offs_t = load_list("offs_t", offs)
-        pos3_t = load_list("pos3_t", pos3)
-        pos1_t = load_list("pos1_t", pos1)
         load_scale_rows(nc.sync, tab_plane, 0, tab_scales)
+        tab_t = [load_table_words("then_below_%d" % a, tab_words[a]) for a in range(2)]
         w1_raw = {(a, 0): load_weight_block(w1, a, 0) for a in range(2)}
 
-        w2_dealt = keep.tile([P, 2 * H], U8, name="w2_dealt", align_bytes=64)
-        nc.vector.tensor_copy(
-            w2_dealt[:].rearrange("p (g t m e) -> p g t m e", g=2, t=PACK, e=2),
-            w2_raw[:].rearrange("p (g m t e) -> p g t m e", g=2, t=PACK, e=2),
-        )
         v2_plane = gather("v2_plane", U8, tab2_plane, offs2_t)
-        v2_words = gather("v2_words", U32, tab2_t, offs2_t)
-        dealt_plane = keep.tile([P, H], U8, name="dealt_plane", align_bytes=64)
-        nc.vector.tensor_copy(
-            dealt_plane[:].rearrange("p (g t m) -> p g t m", g=2, t=PACK),
-            weight_plane[:].rearrange("p (g m t) -> p g t m", g=2, t=PACK),
-        )
         v3_plane = gather("v3_plane", U8, tab3_plane, offs3_t)
+        v2_words = gather("v2_words", U32, tab2_t, offs2_t)
+        w3_q = [quantize_weight_block("w3_0", w3_raw[0], nc.vector.tensor_copy)]
         v3_words = gather("v3_words", U32, tab3_t, offs3_t)
 
-        b_picked = big.tile([P, 8, TESTS], F32, name="big", align_bytes=64)
+        b_picked = big.tile([P, 8, TESTS], F32, name="then_b", align_bytes=64)
         for i in range(8):
             b = first_stage([(
-                w2_dealt[:, 2 * P * i : 2 * P * (i + 1)].bitcast(FP4X4), dealt_plane[:, P * i : P * (i + 1)],
+                w2_raw[:, 2 * P * i : 2 * P * (i + 1)].bitcast(FP4X4), w2_plane[:, P * i : P * (i + 1)],
                 v2_words, v2_plane,
             )])
             nc.vector.tensor_copy(b_picked[:, i, :], b[:].indirect(pos2_t[:]))
 
-        w3_q = [quantize_weight_block("w3_%d" % g, w3_raw[g]) for g in range(2)]
-        for a in range(2):
-            w1_raw[(a, 1)] = load_weight_block(w1, a, 1)
-        v_words = [gather("v_words_%d" % a, U32, tab_t[a], offs_t) for a in range(2)]
+        w3_q.append(quantize_weight_block("w3_1", w3_raw[1], nc.vector.tensor_copy))
+        w1_raw[(0, 1)] = load_weight_block(w1, 0, 1)
+        pos3_t = load_list("pos3_t", pos3)
+        w1_raw[(1, 1)] = load_weight_block(w1, 1, 1)
         v_plane = gather("v_plane", U8, tab_plane, offs_t)
-        d_less_b = big.tile([P, 8, TESTS], F32, name="big", align_bytes=64)
+        v_words = [gather("v_words_%d" % a, U32, tab_t[a], offs_t) for a in range(2)]
+        copies = (nc.vector.tensor_copy, nc.scalar.copy)
+        w1_q = {(a, 0): quantize_weight_block("w1_%d_0" % a, w1_raw[(a, 0)], copies[a]) for a in range(2)}
+        d_less_b = big.tile([P, 8, TESTS], F32, name="then_d", align_bytes=64)
         for i in range(8):
             g, t = divmod(i, PACK)
             cols = slice(P * t, P * (t + 1))
             d = first_stage([(w3_q[g][0][:, cols].bitcast(FP8X4), w3_q[g][1][:, cols], v3_words, v3_plane)])
             nc.vector.tensor_tensor(d_less_b[:, i, :], d[:].indirect(pos3_t[:]), b_picked[:, i, :], ALU.subtract)
 
-        readings = []
-        for g in range(2):
-            w1_q = [quantize_weight_block("w1_%d_%d" % (a, g), w1_raw[(a, g)]) for a in range(2)]
-            for t in range(PACK):
-                cols = slice(P * t, P * (t + 1))
-                readings.append(first_stage([
-                    (w1_q[a][0][:, cols].bitcast(FP8X4), w1_q[a][1][:, cols], v_words[a], v_plane[4 * a :, :])
-                    for a in range(2)
-                ]))
-
         w4_raw = ring.tile([P, 2, N], I32, name="ring", align_bytes=64)
         nc.sync.dma_start(w4_raw[:], w4_words.rearrange("a p c i -> p a (c i)").bitcast(I32))
         load_scale_rows(nc.sync, w4_plane, 0, w4_scales)
+        pos1_t = load_list("pos1_t", pos1)
+
+        homes = [[(keep, name) for name in ("tab2_plane", "tab3_plane", "v2_words", "v3_words")], [(reading, "reading")] * PACK]
+
+        def a_group(g):
+            tiles = []
+            for t in range(PACK):
+                cols = slice(P * t, P * (t + 1))
+                tiles.append(first_stage([
+                    (w1_q[(a, g)][0][:, cols].bitcast(FP8X4), w1_q[(a, g)][1][:, cols], v_words[a], v_plane[4 * a :, :])
+                    for a in range(2)
+                ], *homes[g][t]))
+            below = big.tile([P, PACK, TESTS], F32, name="then_below_%d" % g, align_bytes=64)
+            nc.scalar.activation(below[:], d_less_b[:, PACK * g : PACK * (g + 1), :], RELU, scale=-1.0)
+            return tiles, below
+
+        def spread_unit(h, g, tiles, below):
+            first, width = sum(PIECES[:h]), PIECES[h]
+            tests = slice(first, first + width)
+            offsets = pos1_t[:, first // 16 : (first + width) // 16]
+            blocks = width // P
+            a_less_b = work.tile([P, PACK, width], F32, name="a_less_b", align_bytes=64)
+            for t in range(PACK):
+                nc.vector.tensor_tensor(
+                    a_less_b[:, t, :], tiles[t][:].indirect(offsets), b_picked[:, PACK * g + t, tests], ALU.subtract
+                )
+            high = work.tile([P, PACK, width], F32, name="high", align_bytes=64)
+            nc.vector.scalar_tensor_tensor(
+                high[:], a_less_b[:], 0.0, d_less_b[:, PACK * g : PACK * (g + 1), tests], ALU.max, ALU.max
+            )
+            nc.vector.scalar_tensor_tensor(a_less_b[:], a_less_b[:], -1.0, below[:, :, tests], ALU.mult, ALU.max)
+            spreads = []
+            for c in range(blocks):
+                cols = slice(P * c, P * (c + 1))
+                bank = psum.tile([P, GROUP], F32, name="turned", bufs=2)
+                for t in range(PACK):
+                    turn(bank[:, P * t : P * (t + 1)], [high[:, t, cols], a_less_b[:, t, cols]])
+                spread = work.tile([P, GROUP], BF16, name="spread", align_bytes=64, bufs=4)
+                nc.scalar.copy(
+                    spread[:].rearrange("p (u m e) -> p u m e", u=2, e=2),
+                    bank[:].rearrange("p (m u e) -> p u m e", u=2, e=2),
+                )
+                spreads.append(spread)
+            back = psum.tile([P, blocks, 2, P], F32, name="back", bufs=2)
+            for c in range(blocks):
+                for u in range(2):
+                    turn(back[:, c, u, :], [spreads[c][:].bitcast(F32)[:, P * u : P * (u + 1)]])
+            grouped = rounded.tile([P, PACK * width], BF16, name="rounded", align_bytes=64)
+            nc.scalar.copy(
+                grouped[:].bitcast(F32).rearrange("p (c j u) -> p c j u", c=blocks, u=2),
+                back[:].rearrange("p c u j -> p c j u"),
+            )
+            return quantize("z_%d_%d" % (h, g), grouped[:], width)
+
+        tiles, below = a_group(0)
         w4_dealt_plane = keep.tile([P, N], U8, name="w4_dealt_plane", align_bytes=64)
         nc.vector.tensor_copy(
             w4_dealt_plane[:].rearrange("p (g t m) -> p g t m", g=2, t=PACK),
@@ -187,46 +233,38 @@ def tile_list_chronometer_spread_features_kernel(
             w4_dealt[:].rearrange("p (b t m i) -> p b m t i", b=4, t=PACK, i=4),
             w4_raw[:].rearrange("p a (g m i t) -> p (a g) m t i", g=2, i=4, t=PACK),
         )
+        for a in range(2):
+            w1_q[(a, 1)] = quantize_weight_block("w1_%d_1" % a, w1_raw[(a, 1)], nc.scalar.copy)
+        later_tiles, later_below = a_group(1)
 
         y_codes = keep.tile([P, 2, TESTS], U32, name="y_codes", align_bytes=64)
         y_scales = keep.tile([P, 2, TESTS], U8, name="y_scales", align_bytes=64)
-        for h in range(2):
-            tests = slice(HALF * h, HALF * (h + 1))
-            banks = [psum.tile([P, 2, HALF], F32, name="second") for i in range(4)]
-            for g in range(2):
-                a_less_b = work.tile([P, PACK, HALF], F32, name="a_less_b", align_bytes=64)
-                for t in range(PACK):
-                    i = PACK * g + t
-                    nc.vector.tensor_tensor(
-                        a_less_b[:, t, :], readings[i][:].indirect(pos1_t[:, 16 * h : 16 * (h + 1)]),
-                        b_picked[:, i, tests], ALU.subtract,
-                    )
-                other = d_less_b[:, PACK * g : PACK * (g + 1), tests]
-                high = work.tile([P, PACK, HALF], F32, name="high", align_bytes=64)
-                nc.vector.scalar_tensor_tensor(high[:], a_less_b[:], 0.0, other, ALU.max, ALU.max)
-                nc.vector.scalar_tensor_tensor(a_less_b[:], a_less_b[:], 0.0, other, ALU.min, ALU.min)
-                nc.vector.tensor_tensor(high[:], high[:], a_less_b[:], ALU.subtract)
-                grouped, views = round_interleaved(high[:], HALF)
-                nc.scalar.copy(*views)
-                z_codes, z_scales = quantize("z_%d_%d" % (h, g), grouped[:], HALF)
+        def second_stage(h, z_q):
+            width = PIECES[h]
+            tests = slice(sum(PIECES[:h]), sum(PIECES[: h + 1]))
+            per_bank = BANK // width
+            banks = [psum.tile([P, per_bank, width], F32, name="acc") for i in range(8 // per_bank)]
+            order = (1, 0) if h == 0 else (0, 1)
+            for g in order:
                 for i in range(8):
                     nc.tensor.matmul_mx(
-                        out=banks[i // 2][:, i % 2, :],
+                        out=banks[i // per_bank][:, i % per_bank, :],
                         lhsT=w4_dealt[:, N * g + P * i : N * g + P * (i + 1)].bitcast(FP8X4),
                         lhsT_scale=w4_dealt_plane[4 * g :, P * i : P * (i + 1)],
-                        rhs=z_codes[:].bitcast(FP8X4), rhs_scale=z_scales[:],
-                        start=(g == 0 and i % 2 == 0), stop=(g == 1 and i % 2 == 1),
+                        rhs=z_q[g][0][:].bitcast(FP8X4), rhs_scale=z_q[g][1][:],
+                        start=(g == order[0] and i % per_bank == 0),
+                        stop=(g == order[1] and i % per_bank == per_bank - 1),
                     )
-            y = ring.tile([P, 8, HALF], F32, name="ring", align_bytes=64)
+            y = ring.tile([P, 8, width], F32, name="ring", align_bytes=64)
+            for i, bank in enumerate(banks):
+                nc.scalar.copy(y[:, per_bank * i : per_bank * (i + 1), :], bank[:])
             for g in range(2):
-                for i in (2 * g, 2 * g + 1):
-                    nc.scalar.copy(y[:, 2 * i : 2 * i + 2, :], banks[i][:])
                 y_group = y[:, PACK * g : PACK * (g + 1), :]
                 nc.sync.dma_start(
                     out_0[GROUP * g : GROUP * (g + 1), tests].rearrange("(p t) j -> p t j", t=PACK), y_group
                 )
-                grouped, views = round_interleaved(y_group, HALF)
-                if h == 0:
+                grouped, views = interleave_views(y_group, width)
+                if h < 1:
                     nc.scalar.copy(*views)
                 else:
                     nc.vector.tensor_copy(*views)
@@ -236,6 +274,13 @@ def tile_list_chronometer_spread_features_kernel(
                 nc.sync.dma_start(
                     out_1[g, :, tests, :].rearrange("p m t -> p (m t)").bitcast(I32), y_codes[:, g, tests].bitcast(I32)
                 )
+
+        z_all = []
+        for h in range(len(PIECES)):
+            z_all.append([spread_unit(h, 0, tiles, below), spread_unit(h, 1, later_tiles, later_below)])
+            if h > 0:
+                second_stage(h - 1, z_all[h - 1])
+        second_stage(len(PIECES) - 1, z_all[-1])
         for q in range(4):
             nc.sync.dma_start(
                 out_2[:, 4 * q : 4 * q + 4, :].rearrange("g r m -> r g m").bitcast(I32),

@@ -61,6 +61,10 @@ def tile_list_chronometer_spread_features_kernel(
                     source[:, 4 * q : 4 * q + 4, :].bitcast(I32),
                 )
 
+        def load_one_plane(queue, tile, first_row, source):
+            for r in range(4):
+                queue.dma_start(tile[first_row + r : P : 32, :].bitcast(I32), source[r:16:4, :].bitcast(I32))
+
         def load_weight_block(source, a, g):
             tile = ring.tile([P, PACK, GROUP], F32, name="ring", align_bytes=64)
             rows = source[GROUP * a : GROUP * (a + 1), GROUP * g : GROUP * (g + 1)]
@@ -90,11 +94,8 @@ def tile_list_chronometer_spread_features_kernel(
             copy(*views)
             return quantize(name, grouped[:], GROUP)
 
-        def turn(out, parts):
-            for i, part in enumerate(parts):
-                nc.tensor.matmul(
-                    out, lhsT=part, rhs=identity[:], is_transpose=True, start=(i == 0), stop=(i == len(parts) - 1)
-                )
+        def turn(out, part, start=True, stop=True):
+            nc.tensor.matmul(out, lhsT=part, rhs=identity[:], is_transpose=True, start=start, stop=stop)
 
         def first_stage(passes, pool=reading, name="reading"):
             result = pool.tile([P, S], F32, name=name, align_bytes=64)
@@ -123,17 +124,19 @@ def tile_list_chronometer_spread_features_kernel(
         offs3_t = load_list("offs3_t", offs3)
         w2_raw = keep.tile([P, 2 * H], U8, name="w2_raw", align_bytes=64)
         nc.sync.dma_start(w2_raw[:].bitcast(I32), w2_words[0].bitcast(I32))
-        load_scale_rows(nc.sync, tab2_plane, 0, tab2_scales)
-        load_scale_rows(nc.scalar, tab3_plane, 0, tab3_scales)
-        load_scale_rows(nc.scalar, w2_plane, 0, w2_scales)
+        load_one_plane(nc.sync, tab2_plane, 0, tab2_scales[0])
+        load_one_plane(nc.scalar, tab3_plane, 4, tab3_scales[0])
+        load_one_plane(nc.scalar, w2_plane, 0, w2_scales[0])
         tab2_t = load_table_words("then_b", tab2_words[0])
         w3_raw = [load_weight_block(w3, 0, 0)]
         pos2_t = load_list("pos2_t", pos2)
         tab3_t = load_table_words("then_d", tab3_words[0])
         w3_raw.append(load_weight_block(w3, 0, 1))
         offs_t = load_list("offs_t", offs)
-        load_scale_rows(nc.sync, tab_plane, 0, tab_scales)
-        tab_t = [load_table_words("then_below_%d" % a, tab_words[a]) for a in range(2)]
+        tab_t = []
+        for a in range(2):
+            load_one_plane(nc.sync, tab_plane, 4 * a, tab_scales[a])
+            tab_t.append(load_table_words("then_below_%d" % a, tab_words[a]))
         w1_raw = {(a, 0): load_weight_block(w1, a, 0) for a in range(2)}
 
         v2_plane = gather("v2_plane", U8, tab2_plane, offs2_t)
@@ -158,11 +161,13 @@ def tile_list_chronometer_spread_features_kernel(
         v_words = [gather("v_words_%d" % a, U32, tab_t[a], offs_t) for a in range(2)]
         copies = (nc.vector.tensor_copy, nc.scalar.copy)
         w1_q = {(a, 0): quantize_weight_block("w1_%d_0" % a, w1_raw[(a, 0)], copies[a]) for a in range(2)}
+        for a in range(2):
+            w1_q[(a, 1)] = quantize_weight_block("w1_%d_1" % a, w1_raw[(a, 1)], nc.scalar.copy)
         d_less_b = big.tile([P, 8, TESTS], F32, name="then_d", align_bytes=64)
         for i in range(8):
             g, t = divmod(i, PACK)
             cols = slice(P * t, P * (t + 1))
-            d = first_stage([(w3_q[g][0][:, cols].bitcast(FP8X4), w3_q[g][1][:, cols], v3_words, v3_plane)])
+            d = first_stage([(w3_q[g][0][:, cols].bitcast(FP8X4), w3_q[g][1][:, cols], v3_words, v3_plane[4:, :])])
             nc.vector.tensor_tensor(d_less_b[:, i, :], d[:].indirect(pos3_t[:]), b_picked[:, i, :], ALU.subtract)
 
         w4_raw = ring.tile([P, 2, N], I32, name="ring", align_bytes=64)
@@ -194,7 +199,7 @@ def tile_list_chronometer_spread_features_kernel(
                 nc.vector.tensor_tensor(
                     a_less_b[:, t, :], tiles[t][:].indirect(offsets), b_picked[:, PACK * g + t, tests], ALU.subtract
                 )
-            high = work.tile([P, PACK, width], F32, name="high", align_bytes=64)
+            high = keep.tile([P, PACK, width], F32, name="v_words_%d" % g, align_bytes=64)
             nc.vector.scalar_tensor_tensor(
                 high[:], a_less_b[:], 0.0, d_less_b[:, PACK * g : PACK * (g + 1), tests], ALU.max, ALU.max
             )
@@ -203,8 +208,12 @@ def tile_list_chronometer_spread_features_kernel(
             for c in range(blocks):
                 cols = slice(P * c, P * (c + 1))
                 bank = psum.tile([P, GROUP], F32, name="turned", bufs=2)
-                for t in range(PACK):
-                    turn(bank[:, P * t : P * (t + 1)], [high[:, t, cols], a_less_b[:, t, cols]])
+                for i, term in enumerate((high, a_less_b)):
+                    for t in range(PACK):
+                        turn(
+                            bank[:, P * t : P * (t + 1)], term[:, t, cols],
+                            start=(i == 0 and t == 0), stop=(i == 1 and t == PACK - 1),
+                        )
                 spread = work.tile([P, GROUP], BF16, name="spread", align_bytes=64, bufs=4)
                 nc.scalar.copy(
                     spread[:].rearrange("p (u m e) -> p u m e", u=2, e=2),
@@ -214,7 +223,7 @@ def tile_list_chronometer_spread_features_kernel(
             back = psum.tile([P, blocks, 2, P], F32, name="back", bufs=2)
             for c in range(blocks):
                 for u in range(2):
-                    turn(back[:, c, u, :], [spreads[c][:].bitcast(F32)[:, P * u : P * (u + 1)]])
+                    turn(back[:, c, u, :], spreads[c][:].bitcast(F32)[:, P * u : P * (u + 1)])
             grouped = rounded.tile([P, PACK * width], BF16, name="rounded", align_bytes=64)
             nc.scalar.copy(
                 grouped[:].bitcast(F32).rearrange("p (c j u) -> p c j u", c=blocks, u=2),
@@ -233,8 +242,6 @@ def tile_list_chronometer_spread_features_kernel(
             w4_dealt[:].rearrange("p (b t m i) -> p b m t i", b=4, t=PACK, i=4),
             w4_raw[:].rearrange("p a (g m i t) -> p (a g) m t i", g=2, i=4, t=PACK),
         )
-        for a in range(2):
-            w1_q[(a, 1)] = quantize_weight_block("w1_%d_1" % a, w1_raw[(a, 1)], nc.scalar.copy)
         later_tiles, later_below = a_group(1)
 
         y_codes = keep.tile([P, 2, TESTS], U32, name="y_codes", align_bytes=64)
@@ -282,7 +289,7 @@ def tile_list_chronometer_spread_features_kernel(
                 second_stage(h - 1, z_all[h - 1])
         second_stage(len(PIECES) - 1, z_all[-1])
         for q in range(4):
-            nc.sync.dma_start(
+            nc.scalar.dma_start(
                 out_2[:, 4 * q : 4 * q + 4, :].rearrange("g r m -> r g m").bitcast(I32),
                 y_scales[32 * q : 32 * q + 4, :, :].bitcast(I32),
             )

@@ -19,8 +19,12 @@ RELU = mybir.ActivationFunctionType.Relu
 
 P = 128
 PACK = 4
-GROUP = P * PACK
+PASS = P * PACK
 BANK = 512
+ROW_TILES = H // P
+QUADRANT = 32
+LINE = 4
+ENTRIES_PER_COLUMN = 16
 PIECES = (256, 128, 128)
 
 
@@ -31,85 +35,76 @@ def tile_list_chronometer_spread_features_kernel(
     nc = tc.nc
     with ExitStack() as ctx:
         keep = ctx.enter_context(tc.tile_pool(name="keep", bufs=1))
-        big = ctx.enter_context(tc.tile_pool(name="big", bufs=1))
-        ring = ctx.enter_context(tc.tile_pool(name="ring", bufs=4))
+        tables = ctx.enter_context(tc.tile_pool(name="tables", bufs=1))
+        staging = ctx.enter_context(tc.tile_pool(name="staging", bufs=4))
         rounded = ctx.enter_context(tc.tile_pool(name="rounded", bufs=3))
-        reading = ctx.enter_context(tc.tile_pool(name="reading", bufs=8))
+        readings = ctx.enter_context(tc.tile_pool(name="readings", bufs=ROW_TILES))
         work = ctx.enter_context(tc.tile_pool(name="work", bufs=2))
         psum = ctx.enter_context(tc.psum_pool(name="psum", bufs=4))
 
         def load_list(name, source):
-            tile = keep.tile(list(source.shape), U16, name=name)
-            nc.sync.dma_start(tile[:], source)
-            return tile
+            offsets = keep.tile(list(source.shape), U16, name=name)
+            nc.sync.dma_start(offsets[:], source)
+            return offsets
 
         def load_table_words(name, source):
-            tile = big.tile([P, T], U32, name=name, align_bytes=64)
-            nc.sync.dma_start(tile[:].bitcast(I32), source.rearrange("p t i -> p (t i)").bitcast(I32))
-            return tile
+            words = tables.tile([P, T], U32, name=name, align_bytes=64)
+            nc.sync.dma_start(words[:].bitcast(I32), source.rearrange("p t i -> p (t i)").bitcast(I32))
+            return words
 
         def zeroed_plane(name, width):
-            tile = keep.tile([P, width], U8, name=name, align_bytes=64)
-            nc.vector.memset(tile[:].bitcast(I32), 0)
-            return tile
+            plane = keep.tile([P, width], U8, name=name, align_bytes=64)
+            nc.vector.memset(plane[:].bitcast(I32), 0)
+            return plane
 
-        def load_scale_rows(queue, tile, first_row, source):
-            rows = 4 * source.shape[0]
-            for q in range(4):
-                queue.dma_start(
-                    tile[32 * q + first_row : 32 * q + first_row + rows, :].bitcast(I32),
-                    source[:, 4 * q : 4 * q + 4, :].bitcast(I32),
-                )
-
-        def load_one_plane(queue, tile, first_row, source):
+        def load_scales_of_pass(queue, plane, first_row, source):
             for r in range(4):
-                queue.dma_start(tile[first_row + r : P : 32, :].bitcast(I32), source[r:16:4, :].bitcast(I32))
+                queue.dma_start(plane[first_row + r : P : QUADRANT, :].bitcast(I32), source[r:16:4, :].bitcast(I32))
 
         def load_weight_block(source, a, g):
-            tile = ring.tile([P, PACK, GROUP], F32, name="ring", align_bytes=64)
-            rows = source[GROUP * a : GROUP * (a + 1), GROUP * g : GROUP * (g + 1)]
-            nc.sync.dma_start(tile[:], rows.rearrange("(p j) c -> p j c", j=PACK))
-            return tile
+            raw = staging.tile([P, PACK, PASS], F32, name="weight_block", tag="staged", align_bytes=64)
+            block = source[PASS * a : PASS * (a + 1), PASS * g : PASS * (g + 1)]
+            nc.sync.dma_start(raw[:], block.rearrange("(p t) c -> p t c", t=PACK))
+            return raw
 
-        def gather(name, dtype, table, offsets):
+        def gather_table(name, dtype, window, offsets):
             picked = keep.tile([P, S], dtype, name=name, align_bytes=64)
-            nc.vector.tensor_copy(picked[:], table[:].indirect(offsets[:]))
+            nc.vector.tensor_copy(picked[:], window[:].indirect(offsets[:]))
             return picked
 
-        def quantize(name, values, width):
+        def quantize(name, grouped, width):
             codes = keep.tile([P, width], U32, name=name + "_codes", align_bytes=64)
             scales = keep.tile([P, width], U8, name=name + "_scales", align_bytes=64)
-            nc.vector.quantize_mx(out=codes[:].bitcast(FP8X4), scales=scales[:], in_=values)
+            nc.vector.quantize_mx(out=codes[:].bitcast(FP8X4), scales=scales[:], in_=grouped[:])
             return codes, scales
 
-        def interleave_views(values, width):
-            grouped = rounded.tile([P, PACK * width], BF16, name="rounded", align_bytes=64)
-            return grouped, (
-                grouped[:].rearrange("p (c i t) -> p c t i", i=4, t=PACK),
-                values.rearrange("p t (c i) -> p c t i", i=4),
+        def round_and_group(values, width, copy):
+            grouped = rounded.tile([P, PACK * width], BF16, name="grouped", align_bytes=64)
+            copy(
+                grouped[:].rearrange("p (c i t) -> p c t i", i=LINE, t=PACK),
+                values.rearrange("p t (c i) -> p c t i", i=LINE),
             )
+            return grouped
 
         def quantize_weight_block(name, raw, copy):
-            grouped, views = interleave_views(raw[:], GROUP)
-            copy(*views)
-            return quantize(name, grouped[:], GROUP)
+            return quantize(name, round_and_group(raw[:], PASS, copy), PASS)
 
-        def turn(out, part, start=True, stop=True):
-            nc.tensor.matmul(out, lhsT=part, rhs=identity[:], is_transpose=True, start=start, stop=stop)
+        def turn(out, block, start=True, stop=True):
+            nc.tensor.matmul(out, lhsT=block, rhs=identity[:], is_transpose=True, start=start, stop=stop)
 
-        def first_stage(passes, pool=reading, name="reading"):
-            result = pool.tile([P, S], F32, name=name, align_bytes=64)
+        def first_product(passes, pool, tag):
+            reading = pool.tile([P, S], F32, name="reading", tag=tag, align_bytes=64)
             for c in range(S // BANK):
                 cols = slice(BANK * c, BANK * (c + 1))
-                acc = psum.tile([P, BANK], F32, name="acc")
-                for i, (codes, scales, words, plane) in enumerate(passes):
+                acc = psum.tile([P, BANK], F32, name="first_sum", tag="mx_sum")
+                for i, (weight_codes, weight_scales, table_words, table_plane) in enumerate(passes):
                     nc.tensor.matmul_mx(
-                        out=acc[:], lhsT=codes, lhsT_scale=scales,
-                        rhs=words[:, cols].bitcast(FP8X4), rhs_scale=plane[:, cols],
+                        out=acc[:], lhsT=weight_codes, lhsT_scale=weight_scales,
+                        rhs=table_words[:, cols].bitcast(FP8X4), rhs_scale=table_plane[:, cols],
                         start=(i == 0), stop=(i == len(passes) - 1),
                     )
-                nc.scalar.copy(result[:, cols], acc[:])
-            return result
+                nc.scalar.copy(reading[:, cols], acc[:])
+            return reading
 
         identity = keep.tile([P, P], F32, name="identity")
         make_identity(nc, identity[:])
@@ -120,118 +115,127 @@ def tile_list_chronometer_spread_features_kernel(
         tab_plane = zeroed_plane("tab_plane", T)
         w4_plane = zeroed_plane("w4_plane", N)
 
-        offs2_t = load_list("offs2_t", offs2)
-        offs3_t = load_list("offs3_t", offs3)
-        w2_raw = keep.tile([P, 2 * H], U8, name="w2_raw", align_bytes=64)
-        nc.sync.dma_start(w2_raw[:].bitcast(I32), w2_words[0].bitcast(I32))
-        load_one_plane(nc.sync, tab2_plane, 0, tab2_scales[0])
-        load_one_plane(nc.scalar, tab3_plane, 4, tab3_scales[0])
-        load_one_plane(nc.scalar, w2_plane, 0, w2_scales[0])
-        tab2_t = load_table_words("then_b", tab2_words[0])
+        offs2_list = load_list("offs2_list", offs2)
+        offs3_list = load_list("offs3_list", offs3)
+        w2_codes = keep.tile([P, 2 * H], U8, name="w2_codes", align_bytes=64)
+        nc.sync.dma_start(w2_codes[:].bitcast(I32), w2_words[0].bitcast(I32))
+        load_scales_of_pass(nc.sync, tab2_plane, 0, tab2_scales[0])
+        load_scales_of_pass(nc.scalar, tab3_plane, 4, tab3_scales[0])
+        load_scales_of_pass(nc.scalar, w2_plane, 0, w2_scales[0])
+        tab2_window = load_table_words("tab2_window", tab2_words[0])
         w3_raw = [load_weight_block(w3, 0, 0)]
-        pos2_t = load_list("pos2_t", pos2)
-        tab3_t = load_table_words("then_d", tab3_words[0])
+        pos2_list = load_list("pos2_list", pos2)
+        tab3_window = load_table_words("tab3_window", tab3_words[0])
         w3_raw.append(load_weight_block(w3, 0, 1))
-        offs_t = load_list("offs_t", offs)
-        tab_t = []
+        offs_list = load_list("offs_list", offs)
+        tab_windows = []
         for a in range(2):
-            load_one_plane(nc.sync, tab_plane, 4 * a, tab_scales[a])
-            tab_t.append(load_table_words("then_below_%d" % a, tab_words[a]))
+            load_scales_of_pass(nc.sync, tab_plane, 4 * a, tab_scales[a])
+            tab_windows.append(load_table_words("tab_window_%d" % a, tab_words[a]))
         w1_raw = {(a, 0): load_weight_block(w1, a, 0) for a in range(2)}
 
-        v2_plane = gather("v2_plane", U8, tab2_plane, offs2_t)
-        v3_plane = gather("v3_plane", U8, tab3_plane, offs3_t)
-        v2_words = gather("v2_words", U32, tab2_t, offs2_t)
-        w3_q = [quantize_weight_block("w3_0", w3_raw[0], nc.vector.tensor_copy)]
-        v3_words = gather("v3_words", U32, tab3_t, offs3_t)
+        v2_plane = gather_table("v2_plane", U8, tab2_plane, offs2_list)
+        v3_plane = gather_table("v3_plane", U8, tab3_plane, offs3_list)
+        v2_words = gather_table("v2_words", U32, tab2_window, offs2_list)
+        w3_mx = [quantize_weight_block("w3_0", w3_raw[0], nc.vector.tensor_copy)]
+        v3_words = gather_table("v3_words", U32, tab3_window, offs3_list)
 
-        b_picked = big.tile([P, 8, TESTS], F32, name="then_b", align_bytes=64)
-        for i in range(8):
-            b = first_stage([(
-                w2_raw[:, 2 * P * i : 2 * P * (i + 1)].bitcast(FP4X4), w2_plane[:, P * i : P * (i + 1)],
+        b_picked = tables.tile([P, ROW_TILES, TESTS], F32, name="b_picked", tag="tab2_window", align_bytes=64)
+        for i in range(ROW_TILES):
+            w2_pass = (
+                w2_codes[:, 2 * P * i : 2 * P * (i + 1)].bitcast(FP4X4), w2_plane[:, P * i : P * (i + 1)],
                 v2_words, v2_plane,
-            )])
-            nc.vector.tensor_copy(b_picked[:, i, :], b[:].indirect(pos2_t[:]))
+            )
+            b = first_product([w2_pass], readings, "reading")
+            nc.vector.tensor_copy(b_picked[:, i, :], b[:].indirect(pos2_list[:]))
 
-        w3_q.append(quantize_weight_block("w3_1", w3_raw[1], nc.vector.tensor_copy))
+        w3_mx.append(quantize_weight_block("w3_1", w3_raw[1], nc.vector.tensor_copy))
         w1_raw[(0, 1)] = load_weight_block(w1, 0, 1)
-        pos3_t = load_list("pos3_t", pos3)
+        pos3_list = load_list("pos3_list", pos3)
         w1_raw[(1, 1)] = load_weight_block(w1, 1, 1)
-        v_plane = gather("v_plane", U8, tab_plane, offs_t)
-        v_words = [gather("v_words_%d" % a, U32, tab_t[a], offs_t) for a in range(2)]
-        copies = (nc.vector.tensor_copy, nc.scalar.copy)
-        w1_q = {(a, 0): quantize_weight_block("w1_%d_0" % a, w1_raw[(a, 0)], copies[a]) for a in range(2)}
-        for a in range(2):
-            w1_q[(a, 1)] = quantize_weight_block("w1_%d_1" % a, w1_raw[(a, 1)], nc.scalar.copy)
-        d_less_b = big.tile([P, 8, TESTS], F32, name="then_d", align_bytes=64)
-        for i in range(8):
+        v_plane = gather_table("v_plane", U8, tab_plane, offs_list)
+        v_words = [gather_table("v_words_%d" % a, U32, tab_windows[a], offs_list) for a in range(2)]
+        w1_mx = {}
+        for g in range(2):
+            for a in range(2):
+                copy = nc.vector.tensor_copy if (a, g) == (0, 0) else nc.scalar.copy
+                w1_mx[(a, g)] = quantize_weight_block("w1_%d_%d" % (a, g), w1_raw[(a, g)], copy)
+        d_less_b = tables.tile([P, ROW_TILES, TESTS], F32, name="d_less_b", tag="tab3_window", align_bytes=64)
+        for i in range(ROW_TILES):
             g, t = divmod(i, PACK)
             cols = slice(P * t, P * (t + 1))
-            d = first_stage([(w3_q[g][0][:, cols].bitcast(FP8X4), w3_q[g][1][:, cols], v3_words, v3_plane[4:, :])])
-            nc.vector.tensor_tensor(d_less_b[:, i, :], d[:].indirect(pos3_t[:]), b_picked[:, i, :], ALU.subtract)
+            w3_pass = (w3_mx[g][0][:, cols].bitcast(FP8X4), w3_mx[g][1][:, cols], v3_words, v3_plane[4:, :])
+            d = first_product([w3_pass], readings, "reading")
+            nc.vector.tensor_tensor(d_less_b[:, i, :], d[:].indirect(pos3_list[:]), b_picked[:, i, :], ALU.subtract)
 
-        w4_raw = ring.tile([P, 2, N], I32, name="ring", align_bytes=64)
+        w4_raw = staging.tile([P, 2, N], I32, name="w4_raw", tag="staged", align_bytes=64)
         nc.sync.dma_start(w4_raw[:], w4_words.rearrange("a p c i -> p a (c i)").bitcast(I32))
-        load_scale_rows(nc.sync, w4_plane, 0, w4_scales)
-        pos1_t = load_list("pos1_t", pos1)
+        for q in range(4):
+            nc.sync.dma_start(
+                w4_plane[QUADRANT * q : QUADRANT * q + 8, :].bitcast(I32),
+                w4_scales[:, 4 * q : 4 * q + 4, :].bitcast(I32),
+            )
+        pos1_list = load_list("pos1_list", pos1)
 
-        homes = [[(keep, name) for name in ("tab2_plane", "tab3_plane", "v2_words", "v3_words")], [(reading, "reading")] * PACK]
-
-        def a_group(g):
-            tiles = []
+        def a_rows(g, homes):
+            a_tiles = []
             for t in range(PACK):
                 cols = slice(P * t, P * (t + 1))
-                tiles.append(first_stage([
-                    (w1_q[(a, g)][0][:, cols].bitcast(FP8X4), w1_q[(a, g)][1][:, cols], v_words[a], v_plane[4 * a :, :])
+                w1_passes = [
+                    (w1_mx[(a, g)][0][:, cols].bitcast(FP8X4), w1_mx[(a, g)][1][:, cols], v_words[a], v_plane[4 * a :, :])
                     for a in range(2)
-                ], *homes[g][t]))
-            below = big.tile([P, PACK, TESTS], F32, name="then_below_%d" % g, align_bytes=64)
-            nc.scalar.activation(below[:], d_less_b[:, PACK * g : PACK * (g + 1), :], RELU, scale=-1.0)
-            return tiles, below
+                ]
+                a_tiles.append(first_product(w1_passes, *homes[t]))
+            b_above_d = tables.tile([P, PACK, TESTS], F32, name="b_above_d", tag="tab_window_%d" % g, align_bytes=64)
+            nc.scalar.activation(b_above_d[:], d_less_b[:, PACK * g : PACK * (g + 1), :], RELU, scale=-1.0)
+            return a_tiles, b_above_d
 
-        def spread_unit(h, g, tiles, below):
+        def spread(h, g, a_tiles, b_above_d):
             first, width = sum(PIECES[:h]), PIECES[h]
             tests = slice(first, first + width)
-            offsets = pos1_t[:, first // 16 : (first + width) // 16]
+            offsets = pos1_list[:, first // ENTRIES_PER_COLUMN : (first + width) // ENTRIES_PER_COLUMN]
             blocks = width // P
             a_less_b = work.tile([P, PACK, width], F32, name="a_less_b", align_bytes=64)
             for t in range(PACK):
                 nc.vector.tensor_tensor(
-                    a_less_b[:, t, :], tiles[t][:].indirect(offsets), b_picked[:, PACK * g + t, tests], ALU.subtract
+                    a_less_b[:, t, :], a_tiles[t][:].indirect(offsets), b_picked[:, PACK * g + t, tests], ALU.subtract
                 )
-            high = keep.tile([P, PACK, width], F32, name="v_words_%d" % g, align_bytes=64)
+            above_b = keep.tile([P, PACK, width], F32, name="above_b", tag="v_words_%d" % g, align_bytes=64)
             nc.vector.scalar_tensor_tensor(
-                high[:], a_less_b[:], 0.0, d_less_b[:, PACK * g : PACK * (g + 1), tests], ALU.max, ALU.max
+                above_b[:], a_less_b[:], 0.0, d_less_b[:, PACK * g : PACK * (g + 1), tests], ALU.max, ALU.max
             )
-            nc.vector.scalar_tensor_tensor(a_less_b[:], a_less_b[:], -1.0, below[:, :, tests], ALU.mult, ALU.max)
-            spreads = []
+            below_b = a_less_b
+            nc.vector.scalar_tensor_tensor(below_b[:], a_less_b[:], -1.0, b_above_d[:, :, tests], ALU.mult, ALU.max)
+            z_rows = []
             for c in range(blocks):
                 cols = slice(P * c, P * (c + 1))
-                bank = psum.tile([P, GROUP], F32, name="turned", bufs=2)
-                for i, term in enumerate((high, a_less_b)):
+                z_turned = psum.tile([P, PASS], F32, name="z_turned", bufs=2)
+                for i, term in enumerate((above_b, below_b)):
                     for t in range(PACK):
                         turn(
-                            bank[:, P * t : P * (t + 1)], term[:, t, cols],
+                            z_turned[:, P * t : P * (t + 1)], term[:, t, cols],
                             start=(i == 0 and t == 0), stop=(i == 1 and t == PACK - 1),
                         )
-                spread = work.tile([P, GROUP], BF16, name="spread", align_bytes=64, bufs=4)
+                z_row = work.tile([P, PASS], BF16, name="z_row", align_bytes=64, bufs=4)
                 nc.scalar.copy(
-                    spread[:].rearrange("p (u m e) -> p u m e", u=2, e=2),
-                    bank[:].rearrange("p (m u e) -> p u m e", u=2, e=2),
+                    z_row[:].rearrange("p (u m e) -> p u m e", u=2, e=2),
+                    z_turned[:].rearrange("p (m u e) -> p u m e", u=2, e=2),
                 )
-                spreads.append(spread)
-            back = psum.tile([P, blocks, 2, P], F32, name="back", bufs=2)
+                z_rows.append(z_row)
+            z_words = psum.tile([P, blocks, 2, P], F32, name="z_words", bufs=2)
             for c in range(blocks):
                 for u in range(2):
-                    turn(back[:, c, u, :], spreads[c][:].bitcast(F32)[:, P * u : P * (u + 1)])
-            grouped = rounded.tile([P, PACK * width], BF16, name="rounded", align_bytes=64)
+                    turn(z_words[:, c, u, :], z_rows[c][:].bitcast(F32)[:, P * u : P * (u + 1)])
+            grouped = rounded.tile([P, PACK * width], BF16, name="grouped", align_bytes=64)
             nc.scalar.copy(
                 grouped[:].bitcast(F32).rearrange("p (c j u) -> p c j u", c=blocks, u=2),
-                back[:].rearrange("p c u j -> p c j u"),
+                z_words[:].rearrange("p c u j -> p c j u"),
             )
-            return quantize("z_%d_%d" % (h, g), grouped[:], width)
+            return quantize("z_%d_%d" % (h, g), grouped, width)
 
-        tiles, below = a_group(0)
+        freed = ("tab2_plane", "tab3_plane", "v2_words", "v3_words")
+        a_low = a_rows(0, [(keep, tag) for tag in freed])
+
         w4_dealt_plane = keep.tile([P, N], U8, name="w4_dealt_plane", align_bytes=64)
         nc.vector.tensor_copy(
             w4_dealt_plane[:].rearrange("p (g t m) -> p g t m", g=2, t=PACK),
@@ -239,42 +243,41 @@ def tile_list_chronometer_spread_features_kernel(
         )
         w4_dealt = keep.tile([P, 2 * N], I32, name="w4_dealt", align_bytes=64)
         nc.vector.tensor_copy(
-            w4_dealt[:].rearrange("p (b t m i) -> p b m t i", b=4, t=PACK, i=4),
-            w4_raw[:].rearrange("p a (g m i t) -> p (a g) m t i", g=2, i=4, t=PACK),
+            w4_dealt[:].rearrange("p (b t m i) -> p b m t i", b=4, t=PACK, i=LINE),
+            w4_raw[:].rearrange("p a (g m i t) -> p (a g) m t i", g=2, i=LINE, t=PACK),
         )
-        later_tiles, later_below = a_group(1)
+        a_high = a_rows(1, [(readings, "reading")] * PACK)
 
         y_codes = keep.tile([P, 2, TESTS], U32, name="y_codes", align_bytes=64)
         y_scales = keep.tile([P, 2, TESTS], U8, name="y_scales", align_bytes=64)
-        def second_stage(h, z_q):
+
+        def second_product(h, z_mx):
             width = PIECES[h]
             tests = slice(sum(PIECES[:h]), sum(PIECES[: h + 1]))
             per_bank = BANK // width
-            banks = [psum.tile([P, per_bank, width], F32, name="acc") for i in range(8 // per_bank)]
-            order = (1, 0) if h == 0 else (0, 1)
-            for g in order:
-                for i in range(8):
+            banks = [
+                psum.tile([P, per_bank, width], F32, name="second_sum", tag="mx_sum")
+                for i in range(ROW_TILES // per_bank)
+            ]
+            for a in range(2):
+                for i in range(ROW_TILES):
                     nc.tensor.matmul_mx(
                         out=banks[i // per_bank][:, i % per_bank, :],
-                        lhsT=w4_dealt[:, N * g + P * i : N * g + P * (i + 1)].bitcast(FP8X4),
-                        lhsT_scale=w4_dealt_plane[4 * g :, P * i : P * (i + 1)],
-                        rhs=z_q[g][0][:].bitcast(FP8X4), rhs_scale=z_q[g][1][:],
-                        start=(g == order[0] and i % per_bank == 0),
-                        stop=(g == order[1] and i % per_bank == per_bank - 1),
+                        lhsT=w4_dealt[:, N * a + P * i : N * a + P * (i + 1)].bitcast(FP8X4),
+                        lhsT_scale=w4_dealt_plane[4 * a :, P * i : P * (i + 1)],
+                        rhs=z_mx[a][0][:].bitcast(FP8X4), rhs_scale=z_mx[a][1][:],
+                        start=(a == 0 and i % per_bank == 0),
+                        stop=(a == 1 and i % per_bank == per_bank - 1),
                     )
-            y = ring.tile([P, 8, width], F32, name="ring", align_bytes=64)
+            y = staging.tile([P, ROW_TILES, width], F32, name="y", tag="staged", align_bytes=64)
             for i, bank in enumerate(banks):
                 nc.scalar.copy(y[:, per_bank * i : per_bank * (i + 1), :], bank[:])
             for g in range(2):
-                y_group = y[:, PACK * g : PACK * (g + 1), :]
+                y_pass = y[:, PACK * g : PACK * (g + 1), :]
                 nc.sync.dma_start(
-                    out_0[GROUP * g : GROUP * (g + 1), tests].rearrange("(p t) j -> p t j", t=PACK), y_group
+                    out_0[PASS * g : PASS * (g + 1), tests].rearrange("(p t) j -> p t j", t=PACK), y_pass
                 )
-                grouped, views = interleave_views(y_group, width)
-                if h < 1:
-                    nc.scalar.copy(*views)
-                else:
-                    nc.vector.tensor_copy(*views)
+                grouped = round_and_group(y_pass, width, nc.vector.tensor_copy)
                 nc.vector.quantize_mx(
                     out=y_codes[:, g, tests].bitcast(FP8X4), scales=y_scales[:, g, tests], in_=grouped[:]
                 )
@@ -282,14 +285,15 @@ def tile_list_chronometer_spread_features_kernel(
                     out_1[g, :, tests, :].rearrange("p m t -> p (m t)").bitcast(I32), y_codes[:, g, tests].bitcast(I32)
                 )
 
-        z_all = []
+        z_pieces = []
         for h in range(len(PIECES)):
-            z_all.append([spread_unit(h, 0, tiles, below), spread_unit(h, 1, later_tiles, later_below)])
+            z_pieces.append([spread(h, 0, *a_low), spread(h, 1, *a_high)])
             if h > 0:
-                second_stage(h - 1, z_all[h - 1])
-        second_stage(len(PIECES) - 1, z_all[-1])
+                second_product(h - 1, z_pieces[h - 1])
+        second_product(len(PIECES) - 1, z_pieces[-1])
+
         for q in range(4):
             nc.scalar.dma_start(
                 out_2[:, 4 * q : 4 * q + 4, :].rearrange("g r m -> r g m").bitcast(I32),
-                y_scales[32 * q : 32 * q + 4, :, :].bitcast(I32),
+                y_scales[QUADRANT * q : QUADRANT * q + 4, :, :].bitcast(I32),
             )

@@ -150,16 +150,15 @@ def tile_list_chronometer_spread_features_kernel(
             nc.vector.tensor_copy(b_picked[:, i, :], b[:].indirect(pos2_list[:]))
 
         w3_mx.append(quantize_weight_block("w3_1", w3_raw[1], nc.vector.tensor_copy))
-        w1_raw[(0, 1)] = load_weight_block(w1, 0, 1)
         pos3_list = load_list("pos3_list", pos3)
+        w1_raw[(0, 1)] = load_weight_block(w1, 0, 1)
         w1_raw[(1, 1)] = load_weight_block(w1, 1, 1)
         v_plane = gather_table("v_plane", U8, tab_plane, offs_list)
         v_words = [gather_table("v_words_%d" % a, U32, tab_windows[a], offs_list) for a in range(2)]
         w1_mx = {}
         for g in range(2):
             for a in range(2):
-                copy = nc.vector.tensor_copy if (a, g) == (0, 0) else nc.scalar.copy
-                w1_mx[(a, g)] = quantize_weight_block("w1_%d_%d" % (a, g), w1_raw[(a, g)], copy)
+                w1_mx[(a, g)] = quantize_weight_block("w1_%d_%d" % (a, g), w1_raw[(a, g)], nc.scalar.copy)
         d_less_b = tables.tile([P, ROW_TILES, TESTS], F32, name="d_less_b", tag="tab3_window", align_bytes=64)
         for i in range(ROW_TILES):
             g, t = divmod(i, PACK)
@@ -187,7 +186,8 @@ def tile_list_chronometer_spread_features_kernel(
                 ]
                 a_tiles.append(first_product(w1_passes, *homes[t]))
             b_above_d = tables.tile([P, PACK, TESTS], F32, name="b_above_d", tag="tab_window_%d" % g, align_bytes=64)
-            nc.scalar.activation(b_above_d[:], d_less_b[:, PACK * g : PACK * (g + 1), :], RELU, scale=-1.0)
+            for t in range(PACK):
+                nc.scalar.activation(b_above_d[:, t, :], d_less_b[:, PACK * g + t, :], RELU, scale=-1.0)
             return a_tiles, b_above_d
 
         def spread(h, g, a_tiles, b_above_d):
@@ -277,7 +277,8 @@ def tile_list_chronometer_spread_features_kernel(
                 nc.sync.dma_start(
                     out_0[PASS * g : PASS * (g + 1), tests].rearrange("(p t) j -> p t j", t=PACK), y_pass
                 )
-                grouped = round_and_group(y_pass, width, nc.vector.tensor_copy)
+                copy = nc.scalar.copy if (h, g) == (0, 0) else nc.vector.tensor_copy
+                grouped = round_and_group(y_pass, width, copy)
                 nc.vector.quantize_mx(
                     out=y_codes[:, g, tests].bitcast(FP8X4), scales=y_scales[:, g, tests], in_=grouped[:]
                 )

from contextlib import ExitStack

import concourse.mybir as mybir
from concourse.masks import make_identity

K, K2, H, N, T, S, TESTS = 1024, 512, 1024, 1024, 4096, 1024, 512
FLOPS = 2 * (K + 2 * K2) * H * S + 2 * H * N * TESTS

F32 = mybir.dt.float32
BF16 = mybir.dt.bfloat16
I32 = mybir.dt.int32
U32 = mybir.dt.uint32
U16 = mybir.dt.uint16
U8 = mybir.dt.uint8
FP8X4 = mybir.dt.float8_e4m3fn_x4
FP4X4 = mybir.dt.float4_e2m1fn_x4
ALU = mybir.AluOpType
RELU = mybir.ActivationFunctionType.Relu

P = 128
PACK = 4
PASS = P * PACK
BANK = 512
ROW_TILES = H // P
QUADRANT = 32
LINE = 4
ENTRIES_PER_COLUMN = 16
PIECES = (256, 128, 128)


def tile_list_chronometer_spread_features_kernel(
    tc, tab_words, tab_scales, tab2_words, tab2_scales, tab3_words, tab3_scales, offs, offs2, offs3,
    pos1, pos2, pos3, w1, w2_words, w2_scales, w3, w4_words, w4_scales, out_0, out_1, out_2,
):
    nc = tc.nc
    with ExitStack() as ctx:
        keep = ctx.enter_context(tc.tile_pool(name="keep", bufs=1))
        tables = ctx.enter_context(tc.tile_pool(name="tables", bufs=1))
        staging = ctx.enter_context(tc.tile_pool(name="staging", bufs=4))
        rounded = ctx.enter_context(tc.tile_pool(name="rounded", bufs=3))
        readings = ctx.enter_context(tc.tile_pool(name="readings", bufs=ROW_TILES))
        work = ctx.enter_context(tc.tile_pool(name="work", bufs=2))
        psum = ctx.enter_context(tc.psum_pool(name="psum", bufs=4))

        def load_list(name, source):
            offsets = keep.tile(list(source.shape), U16, name=name)
            nc.sync.dma_start(offsets[:], source)
            return offsets

        def load_table_words(name, source):
            words = tables.tile([P, T], U32, name=name, align_bytes=64)
            nc.sync.dma_start(words[:].bitcast(I32), source.rearrange("p t i -> p (t i)").bitcast(I32))
            return words

        def zeroed_plane(name, width):
            plane = keep.tile([P, width], U8, name=name, align_bytes=64)
            nc.vector.memset(plane[:].bitcast(I32), 0)
            return plane

        def load_scales_of_pass(queue, plane, first_row, source):
            for r in range(4):
                queue.dma_start(plane[first_row + r : P : QUADRANT, :].bitcast(I32), source[r:16:4, :].bitcast(I32))

        def load_weight_block(source, a, g):
            raw = staging.tile([P, PACK, PASS], F32, name="weight_block", tag="staged", align_bytes=64)
            block = source[PASS * a : PASS * (a + 1), PASS * g : PASS * (g + 1)]
            nc.sync.dma_start(raw[:], block.rearrange("(p t) c -> p t c", t=PACK))
            return raw

        def gather_table(name, dtype, window, offsets):
            picked = keep.tile([P, S], dtype, name=name, align_bytes=64)
            nc.vector.tensor_copy(picked[:], window[:].indirect(offsets[:]))
            return picked

        def quantize(name, grouped, width):
            codes = keep.tile([P, width], U32, name=name + "_codes", align_bytes=64)
            scales = keep.tile([P, width], U8, name=name + "_scales", align_bytes=64)
            nc.vector.quantize_mx(out=codes[:].bitcast(FP8X4), scales=scales[:], in_=grouped[:])
            return codes, scales

        def round_and_group(values, width, copy):
            grouped = rounded.tile([P, PACK * width], BF16, name="grouped", align_bytes=64)
            copy(
                grouped[:].rearrange("p (c i t) -> p c t i", i=LINE, t=PACK),
                values.rearrange("p t (c i) -> p c t i", i=LINE),
            )
            return grouped

        def quantize_weight_block(name, raw, copy):
            return quantize(name, round_and_group(raw[:], PASS, copy), PASS)

        def turn(out, block, start=True, stop=True):
            nc.tensor.matmul(out, lhsT=block, rhs=identity[:], is_transpose=True, start=start, stop=stop)

        def first_product(passes, pool, tag):
            reading = pool.tile([P, S], F32, name="reading", tag=tag, align_bytes=64)
            for c in range(S // BANK):
                cols = slice(BANK * c, BANK * (c + 1))
                acc = psum.tile([P, BANK], F32, name="first_sum", tag="mx_sum")
                for i, (weight_codes, weight_scales, table_words, table_plane) in enumerate(passes):
                    nc.tensor.matmul_mx(
                        out=acc[:], lhsT=weight_codes, lhsT_scale=weight_scales,
                        rhs=table_words[:, cols].bitcast(FP8X4), rhs_scale=table_plane[:, cols],
                        start=(i == 0), stop=(i == len(passes) - 1),
                    )
                nc.scalar.copy(reading[:, cols], acc[:])
            return reading

        identity = keep.tile([P, P], F32, name="identity")
        make_identity(nc, identity[:])

        tab2_plane = zeroed_plane("tab2_plane", T)
        tab3_plane = zeroed_plane("tab3_plane", T)
        w2_plane = zeroed_plane("w2_plane", H)
        tab_plane = zeroed_plane("tab_plane", T)
        w4_plane = zeroed_plane("w4_plane", N)

        offs2_list = load_list("offs2_list", offs2)
        offs3_list = load_list("offs3_list", offs3)
        w2_codes = keep.tile([P, 2 * H], U8, name="w2_codes", align_bytes=64)
        nc.sync.dma_start(w2_codes[:].bitcast(I32), w2_words[0].bitcast(I32))
        load_scales_of_pass(nc.sync, tab2_plane, 0, tab2_scales[0])
        load_scales_of_pass(nc.scalar, tab3_plane, 4, tab3_scales[0])
        load_scales_of_pass(nc.scalar, w2_plane, 0, w2_scales[0])
        tab2_window = load_table_words("tab2_window", tab2_words[0])
        w3_raw = [load_weight_block(w3, 0, 0)]
        pos2_list = load_list("pos2_list", pos2)
        tab3_window = load_table_words("tab3_window", tab3_words[0])
        w3_raw.append(load_weight_block(w3, 0, 1))
        offs_list = load_list("offs_list", offs)
        tab_windows = []
        for a in range(2):
            load_scales_of_pass(nc.sync, tab_plane, 4 * a, tab_scales[a])
            tab_windows.append(load_table_words("tab_window_%d" % a, tab_words[a]))
        w1_raw = {(a, 0): load_weight_block(w1, a, 0) for a in range(2)}

        v2_plane = gather_table("v2_plane", U8, tab2_plane, offs2_list)
        v3_plane = gather_table("v3_plane", U8, tab3_plane, offs3_list)
        v2_words = gather_table("v2_words", U32, tab2_window, offs2_list)
        w3_mx = [quantize_weight_block("w3_0", w3_raw[0], nc.vector.tensor_copy)]
        v3_words = gather_table("v3_words", U32, tab3_window, offs3_list)

        b_picked = tables.tile([P, ROW_TILES, TESTS], F32, name="b_picked", tag="tab2_window", align_bytes=64)
        for i in range(ROW_TILES):
            w2_pass = (
                w2_codes[:, 2 * P * i : 2 * P * (i + 1)].bitcast(FP4X4), w2_plane[:, P * i : P * (i + 1)],
                v2_words, v2_plane,
            )
            b = first_product([w2_pass], readings, "reading")
            nc.vector.tensor_copy(b_picked[:, i, :], b[:].indirect(pos2_list[:]))

        w3_mx.append(quantize_weight_block("w3_1", w3_raw[1], nc.vector.tensor_copy))
        pos3_list = load_list("pos3_list", pos3)
        w1_raw[(0, 1)] = load_weight_block(w1, 0, 1)
        w1_raw[(1, 1)] = load_weight_block(w1, 1, 1)
        v_plane = gather_table("v_plane", U8, tab_plane, offs_list)
        v_words = [gather_table("v_words_%d" % a, U32, tab_windows[a], offs_list) for a in range(2)]
        w1_mx = {}
        for g in range(2):
            for a in range(2):
                w1_mx[(a, g)] = quantize_weight_block("w1_%d_%d" % (a, g), w1_raw[(a, g)], nc.scalar.copy)
        d_less_b = tables.tile([P, ROW_TILES, TESTS], F32, name="d_less_b", tag="tab3_window", align_bytes=64)
        for i in range(ROW_TILES):
            g, t = divmod(i, PACK)
            cols = slice(P * t, P * (t + 1))
            w3_pass = (w3_mx[g][0][:, cols].bitcast(FP8X4), w3_mx[g][1][:, cols], v3_words, v3_plane[4:, :])
            d = first_product([w3_pass], readings, "reading")
            nc.vector.tensor_tensor(d_less_b[:, i, :], d[:].indirect(pos3_list[:]), b_picked[:, i, :], ALU.subtract)

        w4_raw = staging.tile([P, 2, N], I32, name="w4_raw", tag="staged", align_bytes=64)
        nc.sync.dma_start(w4_raw[:], w4_words.rearrange("a p c i -> p a (c i)").bitcast(I32))
        for q in range(4):
            nc.sync.dma_start(
                w4_plane[QUADRANT * q : QUADRANT * q + 8, :].bitcast(I32),
                w4_scales[:, 4 * q : 4 * q + 4, :].bitcast(I32),
            )
        pos1_list = load_list("pos1_list", pos1)

        def a_rows(g, homes):
            a_tiles = []
            for t in range(PACK):
                cols = slice(P * t, P * (t + 1))
                w1_passes = [
                    (w1_mx[(a, g)][0][:, cols].bitcast(FP8X4), w1_mx[(a, g)][1][:, cols], v_words[a], v_plane[4 * a :, :])
                    for a in range(2)
                ]
                a_tiles.append(first_product(w1_passes, *homes[t]))
            b_above_d = tables.tile([P, PACK, TESTS], F32, name="b_above_d", tag="tab_window_%d" % g, align_bytes=64)
            for t in range(PACK):
                nc.scalar.activation(b_above_d[:, t, :], d_less_b[:, PACK * g + t, :], RELU, scale=-1.0)
            return a_tiles, b_above_d

        def spread(h, g, a_tiles, b_above_d):
            first, width = sum(PIECES[:h]), PIECES[h]
            tests = slice(first, first + width)
            offsets = pos1_list[:, first // ENTRIES_PER_COLUMN : (first + width) // ENTRIES_PER_COLUMN]
            blocks = width // P
            a_less_b = work.tile([P, PACK, width], F32, name="a_less_b", align_bytes=64)
            for t in range(PACK):
                nc.vector.tensor_tensor(
                    a_less_b[:, t, :], a_tiles[t][:].indirect(offsets), b_picked[:, PACK * g + t, tests], ALU.subtract
                )
            above_b = keep.tile([P, PACK, width], F32, name="above_b", tag="v_words_%d" % g, align_bytes=64)
            nc.vector.scalar_tensor_tensor(
                above_b[:], a_less_b[:], 0.0, d_less_b[:, PACK * g : PACK * (g + 1), tests], ALU.max, ALU.max
            )
            below_b = a_less_b
            nc.vector.scalar_tensor_tensor(below_b[:], a_less_b[:], -1.0, b_above_d[:, :, tests], ALU.mult, ALU.max)
            z_rows = []
            for c in range(blocks):
                cols = slice(P * c, P * (c + 1))
                z_turned = psum.tile([P, PASS], F32, name="z_turned", bufs=2)
                for i, term in enumerate((above_b, below_b)):
                    for t in range(PACK):
                        turn(
                            z_turned[:, P * t : P * (t + 1)], term[:, t, cols],
                            start=(i == 0 and t == 0), stop=(i == 1 and t == PACK - 1),
                        )
                z_row = work.tile([P, PASS], BF16, name="z_row", align_bytes=64, bufs=4)
                nc.scalar.copy(
                    z_row[:].rearrange("p (u m e) -> p u m e", u=2, e=2),
                    z_turned[:].rearrange("p (m u e) -> p u m e", u=2, e=2),
                )
                z_rows.append(z_row)
            z_words = psum.tile([P, blocks, 2, P], F32, name="z_words", bufs=2)
            for c in range(blocks):
                for u in range(2):
                    turn(z_words[:, c, u, :], z_rows[c][:].bitcast(F32)[:, P * u : P * (u + 1)])
            grouped = rounded.tile([P, PACK * width], BF16, name="grouped", align_bytes=64)
            nc.scalar.copy(
                grouped[:].bitcast(F32).rearrange("p (c j u) -> p c j u", c=blocks, u=2),
                z_words[:].rearrange("p c u j -> p c j u"),
            )
            return quantize("z_%d_%d" % (h, g), grouped, width)

        freed = ("tab2_plane", "tab3_plane", "v2_words", "v3_words")
        a_low = a_rows(0, [(keep, tag) for tag in freed])

        w4_dealt_plane = keep.tile([P, N], U8, name="w4_dealt_plane", align_bytes=64)
        nc.vector.tensor_copy(
            w4_dealt_plane[:].rearrange("p (g t m) -> p g t m", g=2, t=PACK),
            w4_plane[:].rearrange("p (g m t) -> p g t m", g=2, t=PACK),
        )
        w4_dealt = keep.tile([P, 2 * N], I32, name="w4_dealt", align_bytes=64)
        nc.vector.tensor_copy(
            w4_dealt[:].rearrange("p (b t m i) -> p b m t i", b=4, t=PACK, i=LINE),
            w4_raw[:].rearrange("p a (g m i t) -> p (a g) m t i", g=2, i=LINE, t=PACK),
        )
        a_high = a_rows(1, [(readings, "reading")] * PACK)

        y_codes = keep.tile([P, 2, TESTS], U32, name="y_codes", align_bytes=64)
        y_scales = keep.tile([P, 2, TESTS], U8, name="y_scales", align_bytes=64)

        def second_product(h, z_mx):
            width = PIECES[h]
            tests = slice(sum(PIECES[:h]), sum(PIECES[: h + 1]))
            per_bank = BANK // width
            banks = [
                psum.tile([P, per_bank, width], F32, name="second_sum", tag="mx_sum")
                for i in range(ROW_TILES // per_bank)
            ]
            for a in range(2):
                for i in range(ROW_TILES):
                    nc.tensor.matmul_mx(
                        out=banks[i // per_bank][:, i % per_bank, :],
                        lhsT=w4_dealt[:, N * a + P * i : N * a + P * (i + 1)].bitcast(FP8X4),
                        lhsT_scale=w4_dealt_plane[4 * a :, P * i : P * (i + 1)],
                        rhs=z_mx[a][0][:].bitcast(FP8X4), rhs_scale=z_mx[a][1][:],
                        start=(a == 0 and i % per_bank == 0),
                        stop=(a == 1 and i % per_bank == per_bank - 1),
                    )
            y = staging.tile([P, ROW_TILES, width], F32, name="y", tag="staged", align_bytes=64)
            for i, bank in enumerate(banks):
                nc.scalar.copy(y[:, per_bank * i : per_bank * (i + 1), :], bank[:])
            for g in range(2):
                y_pass = y[:, PACK * g : PACK * (g + 1), :]
                nc.sync.dma_start(
                    out_0[PASS * g : PASS * (g + 1), tests].rearrange("(p t) j -> p t j", t=PACK), y_pass
                )
                copy = nc.scalar.copy if (h, g) == (0, 0) else nc.vector.tensor_copy
                grouped = round_and_group(y_pass, width, copy)
                nc.vector.quantize_mx(
                    out=y_codes[:, g, tests].bitcast(FP8X4), scales=y_scales[:, g, tests], in_=grouped[:]
                )
                nc.sync.dma_start(
                    out_1[g, :, tests, :].rearrange("p m t -> p (m t)").bitcast(I32), y_codes[:, g, tests].bitcast(I32)
                )

        z_pieces = []
        for h in range(len(PIECES)):
            z_pieces.append([spread(h, 0, *a_low), spread(h, 1, *a_high)])
            if h > 0:
                second_product(h - 1, z_pieces[h - 1])
        second_product(len(PIECES) - 1, z_pieces[-1])

        for q in range(4):
            nc.scalar.dma_start(
                out_2[:, 4 * q : 4 * q + 4, :].rearrange("g r m -> r g m").bitcast(I32),
                y_scales[QUADRANT * q : QUADRANT * q + 4, :, :].bitcast(I32),
            )
